import numpy as np
import ml_dtypes


def mxq(x, axis, fmt="e4m3"):
    dtype, down = {"e4m3": (ml_dtypes.float8_e4m3fn, 7), "e5m2": (ml_dtypes.float8_e5m2, 14)}[fmt]
    v = np.moveaxis(np.asarray(x, np.float32).astype(ml_dtypes.bfloat16).astype(np.float64), axis, -1)
    blocks = v.reshape(v.shape[:-1] + (-1, 32))
    amax = np.abs(blocks).max(-1, keepdims=True)
    byte = np.maximum(np.where(amax > 0, np.frexp(amax)[1] - 1 + 127, 0) - down, 1)
    scale = np.exp2(byte - 127.0)
    codes = (blocks / scale).astype(np.float32).astype(dtype).astype(np.float64)
    return np.moveaxis((codes * scale).reshape(v.shape), -1, axis)


WIDE = False


def mx_kscale(k):
    if not WIDE:
        return np.ones(k)
    levels = np.array([10, -10, 5, -5, 0])
    if k % 512:
        return np.exp2(np.random.permutation(np.resize(levels, k // 32))).repeat(32)
    a = np.empty((k // 512, 16))
    for p in range(k // 512):
        a[p, :8] = np.random.permutation(np.resize(levels, 8))
        for g in range(8):
            far = levels[np.abs(levels - a[p, g]) >= 10]
            a[p, g + 8] = far[np.random.randint(len(far))]
    return np.exp2(a.ravel()).repeat(32)


def f64(x):
    return np.asarray(x).astype(np.float64)


def striped(idx):
    return np.tile(idx.reshape(-1, 16).T, (8, 1)).astype(np.uint16)


def unstriped(offs):
    return offs[:16].T.reshape(-1).astype(np.int64)


E2M1 = np.array([0.0, 0.5, 1.0, 1.5, 2.0, 3.0, 4.0, 6.0, -0.0, -0.5, -1.0, -1.5, -2.0, -3.0, -4.0, -6.0])


def pack_weight(w, fmt):
    k, n = w.shape
    w = f64(np.asarray(w, np.float32).astype(ml_dtypes.bfloat16)).reshape(k // 32, 32, n)
    amax = np.abs(w).max(1)
    if fmt == "e4m3":
        byte = np.frexp(amax)[1] - 1 + 127 - 7
    else:
        mant, ex = np.frexp(amax / 6.0)
        byte = np.where(mant > 0.5, ex, ex - 1) + 127
    byte = np.clip(np.where(amax > 0, byte, 1), 1, 254)
    scaled = (w * np.exp2(127.0 - byte)[:, None, :]).reshape(k, n).astype(np.float32)
    by_word = np.ascontiguousarray(scaled.reshape(k // 512, 128, 4, n).transpose(0, 1, 3, 2))
    if fmt == "e4m3":
        words = by_word.astype(ml_dtypes.float8_e4m3fn).view(np.uint8)
    else:
        c = by_word.astype(ml_dtypes.float4_e2m1fn).view(np.uint8) & 0xF
        words = (c[..., 0::2] | (c[..., 1::2] << 4)).reshape(k // 512, 128, 2 * n)
    return np.ascontiguousarray(words), np.ascontiguousarray(byte.astype(np.uint8).reshape(k // 512, 16, n))


def unpack_weight(words, scales, fmt):
    g, _, n = scales.shape
    words = np.ascontiguousarray(words).reshape(g, 128, n, -1)
    if fmt == "e4m3":
        vals = words.view(ml_dtypes.float8_e4m3fn).astype(np.float64)
    else:
        nib = np.empty((g, 128, n, 4), np.uint8)
        nib[..., 0::2] = words & 0xF
        nib[..., 1::2] = words >> 4
        vals = E2M1[nib]
    vals = vals * np.repeat(np.exp2(scales.astype(np.float64) - 127.0), 8, axis=1)[..., None]
    return vals.transpose(0, 1, 3, 2).reshape(g * 512, n)


def gelu(v):
    return 0.5 * v * (1.0 + np.tanh(np.sqrt(2.0 / np.pi) * (v + 0.044715 * v**3)))


K, H, N, T, S, T2 = 1024, 1024, 768, 2048, 512, 1024

def setup_inputs():
    n = np.random.standard_normal
    s = mx_kscale(K)[:, None]
    u = mx_kscale(H)[:, None]
    tab_words, tab_scales = pack_weight(n((K, T)) * s, "e4m3")
    wa_words, wa_scales = pack_weight(0.35 * n((K, H)) / np.sqrt(K) / s, "e2m1")
    we_words, we_scales = pack_weight(2.0 * n((H, N)) / np.sqrt(H) / u, "e4m3")
    return {
        "tab_words": tab_words, "tab_scales": tab_scales,
        "offs": striped(np.random.permutation(T)[:S]),
        "offs2": striped(np.random.permutation(T)[:S]),
        "offs3": striped(np.random.permutation(T2)[:S]),
        "wa_words": wa_words, "wa_scales": wa_scales,
        "wb": (0.33 * n((K, H)) / np.sqrt(K) / s).astype(np.float32),
        "bh": (0.2 * n(H)).astype(np.float32),
        "gain": (np.exp(0.3 * n(H)) * u[:, 0]).astype(np.float32),
        "wc": (2.0 * n((H, N)) / np.sqrt(H) / u).astype(np.float32),
        "we_words": we_words, "we_scales": we_scales,
        "be": (0.5 * n(N)).astype(np.float32),
        "wgo": np.exp(0.3 * n((128, S))).astype(np.float32),
    }

def reference(tab_words, tab_scales, offs, offs2, offs3, wa_words, wa_scales, wb, bh, gain, wc, we_words, we_scales, be, wgo):
    TW = unpack_weight(tab_words, tab_scales, "e4m3")
    v = TW[:, unstriped(offs)]
    v2 = TW[:, unstriped(offs2)]
    wa = unpack_weight(wa_words, wa_scales, "e2m1")
    we = unpack_weight(we_words, we_scales, "e4m3")
    d = wa.T @ v + mxq(f64(wb), 0, "e4m3").T @ v2
    h = np.sin(d + f64(bh)[:, None]) * f64(gain)[:, None]
    hq = mxq(h, 0, "e4m3")
    yc = mxq(f64(wc), 0, "e4m3").T @ hq
    ye = we.T @ hq
    y = np.maximum(yc, ye + f64(be)[:, None])
    out = np.zeros((N, T2))
    out[:, unstriped(offs3)] = np.tile(f64(wgo), (N // 128, 1)) * y
    return out

@@ -1,0 +1,349 @@
+from contextlib import ExitStack
+
+import concourse.mybir as mybir
+
+K, H, N, T, S, T2 = 1024, 1024, 768, 2048, 512, 1024
+FLOPS = 2 * 2 * K * H * S + 2 * 2 * H * N * S
+
+F32 = mybir.dt.float32
+BF16 = mybir.dt.bfloat16
+I32 = mybir.dt.int32
+U32 = mybir.dt.uint32
+U16 = mybir.dt.uint16
+U8 = mybir.dt.uint8
+FP8X4 = mybir.dt.float8_e4m3fn_x4
+FP4X4 = mybir.dt.float4_e2m1fn_x4
+ACT = mybir.ActivationFunctionType
+ALU = mybir.AluOpType
+
+P = 128
+PACK = 4
+KP = P * PACK
+PASSES = 2
+HALF = S // 2
+CHUNK = 256
+CHUNKS = N // CHUNK
+QUADS = 4
+LINE = 4
+
+
+def tile_list_backhaul_hop_planner_kernel(
+    tc, tab_words, tab_scales, offs, offs2, offs3, wa_words, wa_scales, wb, bh, gain, wc,
+    we_words, we_scales, be, wgo, out,
+):
+    nc = tc.nc
+    with ExitStack() as ctx:
+        lists = ctx.enter_context(tc.tile_pool(name="lists", bufs=1))
+        keep = ctx.enter_context(tc.tile_pool(name="keep", bufs=1))
+        ring = ctx.enter_context(tc.tile_pool(name="ring", bufs=3))
+        psum = ctx.enter_context(tc.psum_pool(name="psum", bufs=1))
+
+        def sb(name, cols, dtype):
+            return keep.tile([P, cols], dtype, name=name, align_bytes=64)
+
+        def bank(number):
+            return psum.tile([P, 512], F32, name="bank%d" % number)
+
+        tab_plane = sb("tab_plane", T, U8)
+        wa_plane_raw = sb("wa_plane_raw", PASSES * H, U8)
+        we_plane = sb("we_plane", N, U8)
+        near_plane1 = sb("near_plane1", S, U8)
+        for plane in (tab_plane, wa_plane_raw, we_plane, near_plane1):
+            nc.vector.memset(plane[:].bitcast(I32), 0)
+        pages = [sb("page%d" % n, T2, F32) for n in range(N // P)]
+        for page in pages:
+            nc.vector.memset(page[:], 0.0)
+
+        near_list = lists.tile([P, S // 16], U16, name="near_list")
+        far_list = lists.tile([P, S // 16], U16, name="far_list")
+        place_list = lists.tile([P, S // 16], U16, name="place_list")
+        tab = [sb("tab%d" % a, T, U32) for a in range(PASSES)]
+
+        def load_tab(a):
+            nc.sync.dma_start(
+                out=tab[a][:].bitcast(I32),
+                in_=tab_words[a].rearrange("p t i -> p (t i)").bitcast(I32),
+            )
+
+        def load_rows(name, w, a, c0, width):
+            raw = sb(name, PACK * width, F32)
+            nc.sync.dma_start(
+                out=raw[:].rearrange("p (j c) -> p j c", j=PACK),
+                in_=w[KP * a : KP * (a + 1), c0 : c0 + width].rearrange("(p j) c -> p j c", j=PACK),
+            )
+            return raw
+
+        nc.sync.dma_start(near_list[:], offs)
+        nc.sync.dma_start(far_list[:], offs2)
+        load_tab(0)
+        nc.sync.dma_start(place_list[:], offs3)
+        bh_cols = sb("bh_cols", 8, F32)
+        gain_cols = sb("gain_cols", 8, F32)
+        for cols, vec in ((bh_cols, bh), (gain_cols, gain)):
+            nc.sync.dma_start(
+                out=cols[:].rearrange("p (b t) -> p b t", t=PACK),
+                in_=vec.rearrange("(b p t) -> p b t", p=P, t=PACK),
+            )
+        wa_raw = [sb("wa_raw%d" % a, 2 * H, U8) for a in range(PASSES)]
+        for a in range(PASSES):
+            nc.sync.dma_start(out=wa_raw[a][:].bitcast(I32), in_=wa_words[a].bitcast(I32))
+        for q in range(QUADS):
+            nc.sync.dma_start(
+                out=tab_plane[32 * q : 32 * q + 8, :].bitcast(I32),
+                in_=tab_scales[:, 4 * q : 4 * q + 4, :].bitcast(I32),
+            )
+        wb_raw = {}
+        wb_raw[0, 0] = [load_rows("wb_raw00", wb, 0, 0, KP)]
+        for q in range(QUADS):
+            nc.sync.dma_start(
+                out=wa_plane_raw[32 * q : 32 * q + 4, :].bitcast(I32).rearrange("r (a c) -> r a c", a=PASSES),
+                in_=wa_scales[:, 4 * q : 4 * q + 4, :].bitcast(I32).rearrange("a r c -> r a c"),
+            )
+        load_tab(1)
+        for q in range(QUADS):
+            nc.sync.dma_start(
+                out=we_plane[32 * q : 32 * q + 8, :].bitcast(I32),
+                in_=we_scales[:, 4 * q : 4 * q + 4, :].bitcast(I32),
+            )
+        wb_raw[0, 1] = [load_rows("wb_raw01", wb, 1, 0, KP)]
+        wb_raw[1, 0] = [load_rows("wb_raw10", wb, 0, KP, KP)]
+        wb_raw[1, 1] = [load_rows("wb_raw11_%d" % u, wb, 1, KP + u * 256, 256) for u in range(2)]
+
+        we_codes = []
+        wc_raw = []
+
+        def load_chunk(c):
+            codes = sb("we_codes%d" % c, PASSES * CHUNK, U32)
+            nc.sync.dma_start(
+                out=codes[:].bitcast(I32).rearrange("p (a c) -> p a c", a=PASSES),
+                in_=we_words[:, :, CHUNK * c : CHUNK * (c + 1), :].rearrange("a p c i -> p a (c i)").bitcast(I32),
+            )
+            we_codes.append(codes)
+            wc_raw.append([load_rows("wc_raw%d%d" % (c, a), wc, a, CHUNK * c, CHUNK) for a in range(PASSES)])
+
+        load_chunk(0)
+        be_cols = sb("be_cols", N // P, F32)
+        with nc.allow_non_contiguous_dma(reason="one bias value for each partition and tile of rows"):
+            nc.sync.dma_start(out=be_cols[:], in_=be.rearrange("(n p) -> p n", p=P))
+        wgo_sb = sb("wgo_sb", S, F32)
+        nc.sync.dma_start(out=wgo_sb[:], in_=wgo)
+        for c in range(1, CHUNKS):
+            load_chunk(c)
+
+        far_plane = sb("far_plane", S, U8)
+        near_plane = sb("near_plane", S, U8)
+        nc.vector.tensor_copy(near_plane[:], tab_plane[:].indirect(near_list[:]))
+        nc.vector.tensor_copy(far_plane[:], tab_plane[:].indirect(far_list[:]))
+        near_planes = [near_plane, near_plane1]
+
+        wa_plane = sb("wa_plane", PASSES * H, U8)
+        nc.vector.tensor_copy(
+            out=wa_plane[:].rearrange("p (g t m) -> p g m t", t=PACK, m=P),
+            in_=wa_plane_raw[:].rearrange("p (g m t) -> p g m t", t=PACK, m=P),
+        )
+        wa_codes = []
+        for a in range(PASSES):
+            codes = sb("wa_codes%d" % a, 2 * H, U8)
+            nc.scalar.copy(
+                out=codes[:].bitcast(U16).rearrange("p (b t m) -> p b m t", t=PACK, m=P),
+                in_=wa_raw[a][:].bitcast(U16).rearrange("p (b m t) -> p b m t", t=PACK, m=P),
+            )
+            wa_codes.append(codes)
+        nc.scalar.dma_start(out=near_plane1[0:100, :].bitcast(I32), in_=near_plane[4:104, :].bitcast(I32))
+
+        near = [sb("near%d" % a, S, U32) for a in range(PASSES)]
+        far = [sb("far%d" % a, S, U32) for a in range(PASSES)]
+
+        def gather_pass(a):
+            nc.vector.tensor_copy(near[a][:], tab[a][:].indirect(near_list[:]))
+            nc.vector.tensor_copy(far[a][:], tab[a][:].indirect(far_list[:]))
+
+        def cast(engine, out_ap, in_ap):
+            if engine == "scalar":
+                nc.scalar.copy(out=out_ap, in_=in_ap)
+            else:
+                nc.vector.tensor_copy(out=out_ap, in_=in_ap)
+
+        wb_codes = {}
+        wb_planes = {}
+
+        def quantize_wb(b, a, scalar_share, calls):
+            woven = sb("wb_woven%d%d" % (b, a), PACK * KP, BF16)
+            dst = woven[:].rearrange("p (t m j) -> p m j t", t=PACK, j=PACK)
+            raws = wb_raw[b, a]
+            per_raw = P // len(raws)
+            for engine, m0, m1 in (("scalar", 0, scalar_share), ("vector", scalar_share, P)):
+                for u, raw in enumerate(raws):
+                    lo, hi = max(m0, u * per_raw), min(m1, (u + 1) * per_raw)
+                    if lo < hi:
+                        src = raw[:].rearrange("p (j m t) -> p m j t", j=PACK, t=PACK)
+                        cast(engine, dst[:, lo:hi], src[:, lo - u * per_raw : hi - u * per_raw])
+            codes = sb("wb_codes%d%d" % (b, a), KP, U32)
+            plane = sb("wb_plane%d%d" % (b, a), KP, U8)
+            width = KP // calls
+            for i in range(calls):
+                cols = slice(i * width, (i + 1) * width)
+                nc.vector.quantize_mx(
+                    out=codes[:, cols].bitcast(FP8X4),
+                    scales=plane[:, cols],
+                    in_=woven[:, PACK * i * width : PACK * (i + 1) * width],
+                )
+            wb_codes[b, a] = codes
+            wb_planes[b, a] = plane
+
+        sums = {(b, u, tp): bank(4 * b + 2 * u + tp) for b in range(PASSES) for u in range(2) for tp in range(2)}
+
+        def near_passes(b, a):
+            for u in range(2):
+                hops = slice(HALF * u, HALF * (u + 1))
+                for t in range(PACK):
+                    c0 = KP * b + P * t
+                    nc.tensor.matmul_mx(
+                        out=sums[b, u, t // 2][:, HALF * (t % 2) : HALF * (t % 2 + 1)],
+                        lhsT=wa_codes[a][:, 2 * c0 : 2 * (c0 + P)].bitcast(FP4X4),
+                        lhsT_scale=wa_plane[:, H * a + c0 : H * a + c0 + P],
+                        rhs=near[a][:, hops].bitcast(FP8X4),
+                        rhs_scale=near_planes[a][:, hops],
+                        start=(a == 0 and t % 2 == 0),
+                        stop=False,
+                    )
+
+        def far_passes(b, a):
+            for u in range(2):
+                hops = slice(HALF * u, HALF * (u + 1))
+                for t in range(PACK):
+                    cols = slice(P * t, P * (t + 1))
+                    nc.tensor.matmul_mx(
+                        out=sums[b, u, t // 2][:, HALF * (t % 2) : HALF * (t % 2 + 1)],
+                        lhsT=wb_codes[b, a][:, cols].bitcast(FP8X4),
+                        lhsT_scale=wb_planes[b, a][:, cols],
+                        rhs=far[a][:, hops].bitcast(FP8X4),
+                        rhs_scale=far_plane[4 * a : P, hops],
+                        start=False,
+                        stop=(a == PASSES - 1 and t % 2 == 1),
+                    )
+
+        h_codes = [sb("h_codes%d" % b, S, U32) for b in range(PASSES)]
+        h_planes = [sb("h_plane%d" % b, S, U8) for b in range(PASSES)]
+
+        def features(b, u):
+            sines = sb("sines%d%d" % (b, u), PACK * HALF, F32)
+            for t in range(PACK):
+                nc.scalar.activation(
+                    out=sines[:, HALF * t : HALF * (t + 1)],
+                    in_=sums[b, u, t // 2][:, HALF * (t % 2) : HALF * (t % 2 + 1)],
+                    func=ACT.Sin,
+                    bias=bh_cols[:, PACK * b + t : PACK * b + t + 1],
+                )
+            woven = sb("h_woven%d%d" % (b, u), PACK * HALF, BF16)
+            gains = gain_cols[:, PACK * b : PACK * (b + 1)].unsqueeze(1).unsqueeze(3)
+            nc.vector.tensor_tensor(
+                out=woven[:].rearrange("p (c i t) -> p c t i", i=LINE, t=PACK),
+                in0=sines[:].rearrange("p (t c i) -> p c t i", i=LINE, t=PACK),
+                in1=gains.to_broadcast([P, HALF // LINE, PACK, LINE]),
+                op=ALU.mult,
+            )
+            hops = slice(HALF * u, HALF * (u + 1))
+            nc.vector.quantize_mx(out=h_codes[b][:, hops].bitcast(FP8X4), scales=h_planes[b][:, hops], in_=woven[:])
+
+        gather_pass(0)
+        near_passes(0, 0)
+        near_passes(1, 0)
+        quantize_wb(0, 0, P, 1)
+        far_passes(0, 0)
+        gather_pass(1)
+        near_passes(0, 1)
+        near_passes(1, 1)
+        quantize_wb(0, 1, P // 2, 1)
+        far_passes(0, 1)
+        quantize_wb(1, 0, P // 2, 1)
+        far_passes(1, 0)
+        features(0, 0)
+        quantize_wb(1, 1, P // 2, PACK)
+        far_passes(1, 1)
+        features(1, 0)
+        features(0, 1)
+
+        wc_codes = {}
+        wc_planes = {}
+
+        def quantize_wc(c, engines):
+            for a in range(PASSES):
+                woven = sb("wc_woven%d%d" % (c, a), PACK * CHUNK, BF16)
+                cast(
+                    engines[a],
+                    woven[:].rearrange("p (c i j) -> p c j i", i=LINE, j=PACK),
+                    wc_raw[c][a][:].rearrange("p (j c i) -> p c j i", i=LINE, j=PACK),
+                )
+                codes = sb("wc_codes%d%d" % (c, a), CHUNK, U32)
+                plane = sb("wc_plane%d%d" % (c, a), CHUNK, U8)
+                nc.vector.quantize_mx(out=codes[:].bitcast(FP8X4), scales=plane[:], in_=woven[:])
+                wc_codes[c, a] = codes
+                wc_planes[c, a] = plane
+
+        def readings(n, j0, width, yc, ye, one_group):
+            c, cols = n // 2, slice(P * (n % 2), P * (n % 2 + 1))
+            hops = slice(j0, j0 + width)
+            for a in range(PASSES):
+                nc.tensor.matmul_mx(
+                    out=ye,
+                    lhsT=we_codes[c][:, CHUNK * a + cols.start : CHUNK * a + cols.stop].bitcast(FP8X4),
+                    lhsT_scale=we_plane[4 * a : P, P * n : P * (n + 1)],
+                    rhs=h_codes[a][:, hops].bitcast(FP8X4),
+                    rhs_scale=h_planes[a][:, hops],
+                    start=(a == 0),
+                    stop=(a == PASSES - 1 and not one_group),
+                )
+                nc.tensor.matmul_mx(
+                    out=yc,
+                    lhsT=wc_codes[c, a][:, cols].bitcast(FP8X4),
+                    lhsT_scale=wc_planes[c, a][:, cols],
+                    rhs=h_codes[a][:, hops].bitcast(FP8X4),
+                    rhs_scale=h_planes[a][:, hops],
+                    start=(a == 0 and not one_group),
+                    stop=(a == PASSES - 1),
+                )
+            biased = ring.tile([P, width], F32, name="biased")
+            nc.scalar.activation(out=biased[:], in_=ye, func=ACT.Identity, bias=be_cols[:, n : n + 1])
+            score = ring.tile([P, width], F32, name="score")
+            nc.vector.tensor_tensor(out=score[:], in0=yc, in1=biased[:], op=ALU.max)
+            return score
+
+        def place(n, j0, width, score):
+            nc.vector.tensor_tensor(
+                out=pages[n][:].indirect(place_list[:, j0 // 16 : (j0 + width) // 16]),
+                in0=score[:],
+                in1=wgo_sb[:, j0 : j0 + width],
+                op=ALU.mult,
+            )
+            if j0 + width == S:
+                nc.sync.dma_start(out=out[P * n : P * (n + 1), :], in_=pages[n][:])
+
+        def half_step(n, u):
+            shared = bank(2 * u + n)
+            return (n, HALF * u, HALF, readings(n, HALF * u, HALF, shared[:, 0:HALF], shared[:, HALF:S], True))
+
+        def whole_step(n):
+            first = (4 + 2 * (n - 2)) % 8
+            return (n, 0, S, readings(n, 0, S, bank(first)[:], bank(first + 1)[:], False))
+
+        quantize_wc(0, ("scalar", "vector"))
+        pending = half_step(0, 0)
+        later = [
+            lambda: half_step(1, 0),
+            lambda: features(1, 1),
+            lambda: half_step(0, 1),
+            lambda: quantize_wc(1, ("scalar", "scalar")),
+            lambda: half_step(1, 1),
+            lambda: whole_step(2),
+            lambda: quantize_wc(2, ("scalar", "scalar")),
+            lambda: whole_step(3),
+            lambda: whole_step(4),
+            lambda: whole_step(5),
+        ]
+        for step in later:
+            made = step()
+            if made is not None:
+                place(*pending)
+                pending = made
+        place(*pending)

@@ -35,24 +35,28 @@ def tile_list_backhaul_hop_planner_kernel(
     with ExitStack() as ctx:
         lists = ctx.enter_context(tc.tile_pool(name="lists", bufs=1))
         keep = ctx.enter_context(tc.tile_pool(name="keep", bufs=1))
+        overlay = ctx.enter_context(tc.tile_pool(name="overlay", bufs=1))
         ring = ctx.enter_context(tc.tile_pool(name="ring", bufs=3))
         psum = ctx.enter_context(tc.psum_pool(name="psum", bufs=1))
 
-        def sb(name, cols, dtype):
-            return keep.tile([P, cols], dtype, name=name, align_bytes=64)
+        def sb(name, cols, dtype, tag=""):
+            return keep.tile([P, cols], dtype, name=name, tag=tag, align_bytes=64)
+
+        def laid_over(name, cols, dtype, offset):
+            return overlay.tile([P, cols], dtype, name=name, offset=offset, align_bytes=64)
 
         def bank(number):
             return psum.tile([P, 512], F32, name="bank%d" % number)
 
         tab_plane = sb("tab_plane", T, U8)
-        wa_plane_raw = sb("wa_plane_raw", PASSES * H, U8)
+        tab_plane1 = sb("tab_plane1", T, U8)
+        wa_plane_raw = laid_over("wa_plane_raw", PASSES * H, U8, 1536)
         we_plane = sb("we_plane", N, U8)
-        near_plane1 = sb("near_plane1", S, U8)
-        for plane in (tab_plane, wa_plane_raw, we_plane, near_plane1):
+        for plane in (tab_plane, wa_plane_raw, tab_plane1, we_plane):
             nc.vector.memset(plane[:].bitcast(I32), 0)
         pages = [sb("page%d" % n, T2, F32) for n in range(N // P)]
         for page in pages:
-            nc.vector.memset(page[:], 0.0)
+            nc.vector.memset(page[:].bitcast(I32), 0)
 
         near_list = lists.tile([P, S // 16], U16, name="near_list")
         far_list = lists.tile([P, S // 16], U16, name="far_list")
@@ -65,8 +69,11 @@ def tile_list_backhaul_hop_planner_kernel(
                 in_=tab_words[a].rearrange("p t i -> p (t i)").bitcast(I32),
             )
 
-        def load_rows(name, w, a, c0, width):
-            raw = sb(name, PACK * width, F32)
+        def load_rows(name, w, a, c0, width, offset=None):
+            if offset is None:
+                raw = sb(name, PACK * width, F32)
+            else:
+                raw = laid_over(name, PACK * width, F32, offset)
             nc.sync.dma_start(
                 out=raw[:].rearrange("p (j c) -> p j c", j=PACK),
                 in_=w[KP * a : KP * (a + 1), c0 : c0 + width].rearrange("(p j) c -> p j c", j=PACK),
@@ -76,14 +83,6 @@ def tile_list_backhaul_hop_planner_kernel(
         nc.sync.dma_start(near_list[:], offs)
         nc.sync.dma_start(far_list[:], offs2)
         load_tab(0)
-        nc.sync.dma_start(place_list[:], offs3)
-        bh_cols = sb("bh_cols", 8, F32)
-        gain_cols = sb("gain_cols", 8, F32)
-        for cols, vec in ((bh_cols, bh), (gain_cols, gain)):
-            nc.sync.dma_start(
-                out=cols[:].rearrange("p (b t) -> p b t", t=PACK),
-                in_=vec.rearrange("(b p t) -> p b t", p=P, t=PACK),
-            )
         wa_raw = [sb("wa_raw%d" % a, 2 * H, U8) for a in range(PASSES)]
         for a in range(PASSES):
             nc.sync.dma_start(out=wa_raw[a][:].bitcast(I32), in_=wa_words[a].bitcast(I32))
@@ -100,14 +99,21 @@ def tile_list_backhaul_hop_planner_kernel(
                 in_=wa_scales[:, 4 * q : 4 * q + 4, :].bitcast(I32).rearrange("a r c -> r a c"),
             )
         load_tab(1)
+        wb_raw[0, 1] = [load_rows("wb_raw01", wb, 1, 0, KP)]
         for q in range(QUADS):
             nc.sync.dma_start(
-                out=we_plane[32 * q : 32 * q + 8, :].bitcast(I32),
-                in_=we_scales[:, 4 * q : 4 * q + 4, :].bitcast(I32),
+                out=tab_plane1[32 * q : 32 * q + 4, :].bitcast(I32),
+                in_=tab_scales[1, 4 * q : 4 * q + 4, :].bitcast(I32),
             )
-        wb_raw[0, 1] = [load_rows("wb_raw01", wb, 1, 0, KP)]
-        wb_raw[1, 0] = [load_rows("wb_raw10", wb, 0, KP, KP)]
+        wb_raw[1, 0] = [load_rows("wb_raw10", wb, 0, KP, KP, 8192)]
         wb_raw[1, 1] = [load_rows("wb_raw11_%d" % u, wb, 1, KP + u * 256, 256) for u in range(2)]
+        bh_cols = sb("bh_cols", 8, F32)
+        gain_cols = sb("gain_cols", 8, F32)
+        for cols, vec in ((bh_cols, bh), (gain_cols, gain)):
+            nc.sync.dma_start(
+                out=cols[:].rearrange("p (b t) -> p b t", t=PACK),
+                in_=vec.rearrange("(b p t) -> p b t", p=P, t=PACK),
+            )
 
         we_codes = []
         wc_raw = []
@@ -121,7 +127,13 @@ def tile_list_backhaul_hop_planner_kernel(
             we_codes.append(codes)
             wc_raw.append([load_rows("wc_raw%d%d" % (c, a), wc, a, CHUNK * c, CHUNK) for a in range(PASSES)])
 
+        for q in range(QUADS):
+            nc.sync.dma_start(
+                out=we_plane[32 * q : 32 * q + 8, :].bitcast(I32),
+                in_=we_scales[:, 4 * q : 4 * q + 4, :].bitcast(I32),
+            )
         load_chunk(0)
+        nc.sync.dma_start(place_list[:], offs3)
         be_cols = sb("be_cols", N // P, F32)
         with nc.allow_non_contiguous_dma(reason="one bias value for each partition and tile of rows"):
             nc.sync.dma_start(out=be_cols[:], in_=be.rearrange("(n p) -> p n", p=P))
@@ -134,6 +146,7 @@ def tile_list_backhaul_hop_planner_kernel(
         near_plane = sb("near_plane", S, U8)
         nc.vector.tensor_copy(near_plane[:], tab_plane[:].indirect(near_list[:]))
         nc.vector.tensor_copy(far_plane[:], tab_plane[:].indirect(far_list[:]))
+        near_plane1 = sb("near_plane1", S, U8)
         near_planes = [near_plane, near_plane1]
 
         wa_plane = sb("wa_plane", PASSES * H, U8)
@@ -149,10 +162,9 @@ def tile_list_backhaul_hop_planner_kernel(
                 in_=wa_raw[a][:].bitcast(U16).rearrange("p (b m t) -> p b m t", t=PACK, m=P),
             )
             wa_codes.append(codes)
-        nc.scalar.dma_start(out=near_plane1[0:100, :].bitcast(I32), in_=near_plane[4:104, :].bitcast(I32))
 
-        near = [sb("near%d" % a, S, U32) for a in range(PASSES)]
-        far = [sb("far%d" % a, S, U32) for a in range(PASSES)]
+        near = [sb("near0", S, U32), laid_over("near1", S, U32, 0)]
+        far = [sb("far0", S, U32), laid_over("far1", S, U32, 2560)]
 
         def gather_pass(a):
             nc.vector.tensor_copy(near[a][:], tab[a][:].indirect(near_list[:]))
@@ -168,7 +180,7 @@ def tile_list_backhaul_hop_planner_kernel(
         wb_planes = {}
 
         def quantize_wb(b, a, scalar_share, calls):
-            woven = sb("wb_woven%d%d" % (b, a), PACK * KP, BF16)
+            woven = sb("wb_woven%d%d" % (b, a), PACK * KP, BF16, tag="wb_woven%d_bytes" % a)
             dst = woven[:].rearrange("p (t m j) -> p m j t", t=PACK, j=PACK)
             raws = wb_raw[b, a]
             per_raw = P // len(raws)
@@ -178,8 +190,11 @@ def tile_list_backhaul_hop_planner_kernel(
                     if lo < hi:
                         src = raw[:].rearrange("p (j m t) -> p m j t", j=PACK, t=PACK)
                         cast(engine, dst[:, lo:hi], src[:, lo - u * per_raw : hi - u * per_raw])
-            codes = sb("wb_codes%d%d" % (b, a), KP, U32)
-            plane = sb("wb_plane%d%d" % (b, a), KP, U8)
+            codes = sb("wb_codes%d%d" % (b, a), KP, U32, tag="wb_codes%d%d_bytes" % (b, a))
+            if (b, a) == (0, 0):
+                plane = laid_over("wb_plane00", KP, U8, 2048)
+            else:
+                plane = sb("wb_plane%d%d" % (b, a), KP, U8)
             width = KP // calls
             for i in range(calls):
                 cols = slice(i * width, (i + 1) * width)
@@ -193,8 +208,8 @@ def tile_list_backhaul_hop_planner_kernel(
 
         sums = {(b, u, tp): bank(4 * b + 2 * u + tp) for b in range(PASSES) for u in range(2) for tp in range(2)}
 
-        def near_passes(b, a):
-            for u in range(2):
+        def near_passes(b, a, u):
+            if True:
                 hops = slice(HALF * u, HALF * (u + 1))
                 for t in range(PACK):
                     c0 = KP * b + P * t
@@ -208,8 +223,8 @@ def tile_list_backhaul_hop_planner_kernel(
                         stop=False,
                     )
 
-        def far_passes(b, a):
-            for u in range(2):
+        def far_passes(b, a, u):
+            if True:
                 hops = slice(HALF * u, HALF * (u + 1))
                 for t in range(PACK):
                     cols = slice(P * t, P * (t + 1))
@@ -226,8 +241,13 @@ def tile_list_backhaul_hop_planner_kernel(
         h_codes = [sb("h_codes%d" % b, S, U32) for b in range(PASSES)]
         h_planes = [sb("h_plane%d" % b, S, U8) for b in range(PASSES)]
 
-        def features(b, u):
-            sines = sb("sines%d%d" % (b, u), PACK * HALF, F32)
+        h_woven = {}
+
+        def weave_features(b, u):
+            if b == 0:
+                sines = laid_over("sines0%d" % u, PACK * HALF, F32, 8192 + 4096 * u)
+            else:
+                sines = sb("sines1%d" % u, PACK * HALF, F32, tag="sines1%d_bytes" % u)
             for t in range(PACK):
                 nc.scalar.activation(
                     out=sines[:, HALF * t : HALF * (t + 1)],
@@ -235,7 +255,7 @@ def tile_list_backhaul_hop_planner_kernel(
                     func=ACT.Sin,
                     bias=bh_cols[:, PACK * b + t : PACK * b + t + 1],
                 )
-            woven = sb("h_woven%d%d" % (b, u), PACK * HALF, BF16)
+            woven = sb("h_woven%d%d" % (b, u), PACK * HALF, BF16, tag="h_woven%d%d_bytes" % (b, u))
             gains = gain_cols[:, PACK * b : PACK * (b + 1)].unsqueeze(1).unsqueeze(3)
             nc.vector.tensor_tensor(
                 out=woven[:].rearrange("p (c i t) -> p c t i", i=LINE, t=PACK),
@@ -243,33 +263,61 @@ def tile_list_backhaul_hop_planner_kernel(
                 in1=gains.to_broadcast([P, HALF // LINE, PACK, LINE]),
                 op=ALU.mult,
             )
+            h_woven[b, u] = woven
+
+        def quantize_features(b, u):
             hops = slice(HALF * u, HALF * (u + 1))
-            nc.vector.quantize_mx(out=h_codes[b][:, hops].bitcast(FP8X4), scales=h_planes[b][:, hops], in_=woven[:])
+            nc.vector.quantize_mx(
+                out=h_codes[b][:, hops].bitcast(FP8X4), scales=h_planes[b][:, hops], in_=h_woven[b, u][:]
+            )
 
         gather_pass(0)
-        near_passes(0, 0)
-        near_passes(1, 0)
+        near_passes(0, 0, 0)
+        near_passes(1, 0, 0)
         quantize_wb(0, 0, P, 1)
-        far_passes(0, 0)
+        far_passes(0, 0, 0)
         gather_pass(1)
-        near_passes(0, 1)
-        near_passes(1, 1)
-        quantize_wb(0, 1, P // 2, 1)
-        far_passes(0, 1)
-        quantize_wb(1, 0, P // 2, 1)
-        far_passes(1, 0)
-        features(0, 0)
-        quantize_wb(1, 1, P // 2, PACK)
-        far_passes(1, 1)
-        features(1, 0)
-        features(0, 1)
+        nc.vector.tensor_copy(near_plane1[:], tab_plane1[:].indirect(near_list[:]))
+        near_passes(0, 1, 0)
+        near_passes(1, 1, 0)
+        quantize_wb(0, 1, P, 1)
+        far_passes(0, 1, 0)
+        quantize_wb(1, 0, P, 1)
+        far_passes(1, 0, 0)
+        quantize_wb(1, 1, 0, PACK)
+        far_passes(1, 1, 0)
+        for b in range(PASSES):
+            weave_features(b, 0)
+        for b in range(PASSES):
+            quantize_features(b, 0)
+        for b in range(PASSES):
+            for a in range(PASSES):
+                near_passes(b, a, 1)
+                far_passes(b, a, 1)
 
         wc_codes = {}
         wc_planes = {}
+        woven_tags = {
+            (0, 0): "",
+            (0, 1): "",
+            (1, 0): "sines10_bytes",
+            (1, 1): "sines11_bytes",
+            (2, 0): "h_woven01_bytes",
+            (2, 1): "h_woven11_bytes",
+        }
+        score_tags = {
+            (0, 0): "h_woven01_bytes",
+            (1, 0): "h_woven11_bytes",
+            (0, 1): "sines10_bytes",
+            (1, 1): "sines11_bytes",
+            (2, 1): "h_woven01_bytes",
+            (3, 1): "h_woven11_bytes",
+        }
 
         def quantize_wc(c, engines):
             for a in range(PASSES):
-                woven = sb("wc_woven%d%d" % (c, a), PACK * CHUNK, BF16)
+                if True:
+                    woven = sb("wc_woven%d%d" % (c, a), PACK * CHUNK, BF16, tag=woven_tags[c, a])
                 cast(
                     engines[a],
                     woven[:].rearrange("p (c i j) -> p c j i", i=LINE, j=PACK),
@@ -281,69 +329,68 @@ def tile_list_backhaul_hop_planner_kernel(
                 wc_codes[c, a] = codes
                 wc_planes[c, a] = plane
 
-        def readings(n, j0, width, yc, ye, one_group):
-            c, cols = n // 2, slice(P * (n % 2), P * (n % 2 + 1))
-            hops = slice(j0, j0 + width)
+        def score_and_place(c, u):
+            hops = slice(HALF * u, HALF * (u + 1))
+            first_bank = (2 * (2 * c + u)) % 8
+            ye, yc = bank(first_bank), bank(first_bank + 1)
             for a in range(PASSES):
-                nc.tensor.matmul_mx(
-                    out=ye,
-                    lhsT=we_codes[c][:, CHUNK * a + cols.start : CHUNK * a + cols.stop].bitcast(FP8X4),
-                    lhsT_scale=we_plane[4 * a : P, P * n : P * (n + 1)],
-                    rhs=h_codes[a][:, hops].bitcast(FP8X4),
-                    rhs_scale=h_planes[a][:, hops],
-                    start=(a == 0),
-                    stop=(a == PASSES - 1 and not one_group),
+                for i in range(2):
+                    n, cols = 2 * c + i, slice(P * i, P * (i + 1))
+                    first, last = (a == 0 and i == 0), (a == PASSES - 1 and i == 1)
+                    nc.tensor.matmul_mx(
+                        out=yc[:, HALF * i : HALF * (i + 1)],
+                        lhsT=wc_codes[c, a][:, cols].bitcast(FP8X4),
+                        lhsT_scale=wc_planes[c, a][:, cols],
+                        rhs=h_codes[a][:, hops].bitcast(FP8X4),
+                        rhs_scale=h_planes[a][:, hops],
+                        start=first,
+                        stop=last,
+                    )
+                for i in range(2):
+                    n, cols = 2 * c + i, slice(P * i, P * (i + 1))
+                    first, last = (a == 0 and i == 0), (a == PASSES - 1 and i == 1)
+                    nc.tensor.matmul_mx(
+                        out=ye[:, HALF * i : HALF * (i + 1)],
+                        lhsT=we_codes[c][:, CHUNK * a + cols.start : CHUNK * a + cols.stop].bitcast(FP8X4),
+                        lhsT_scale=we_plane[4 * a : P, P * n : P * (n + 1)],
+                        rhs=h_codes[a][:, hops].bitcast(FP8X4),
+                        rhs_scale=h_planes[a][:, hops],
+                        start=first,
+                        stop=last,
+                    )
+            yc_sb = ring.tile([P, S], F32, name="yc_sb")
+            nc.scalar.copy(out=yc_sb[:], in_=yc[:])
+            scores = []
+            for i in range(2):
+                n = 2 * c + i
+                score = sb("score%d%d" % (n, u), HALF, F32, tag=score_tags.get((n, u), ""))
+                nc.vector.scalar_tensor_tensor(
+                    out=score[:],
+                    in0=ye[:, HALF * i : HALF * (i + 1)],
+                    scalar=be_cols[:, n : n + 1],
+                    in1=yc_sb[:, HALF * i : HALF * (i + 1)],
+                    op0=ALU.add,
+                    op1=ALU.max,
                 )
-                nc.tensor.matmul_mx(
-                    out=yc,
-                    lhsT=wc_codes[c, a][:, cols].bitcast(FP8X4),
-                    lhsT_scale=wc_planes[c, a][:, cols],
-                    rhs=h_codes[a][:, hops].bitcast(FP8X4),
-                    rhs_scale=h_planes[a][:, hops],
-                    start=(a == 0 and not one_group),
-                    stop=(a == PASSES - 1),
+                scores.append(score)
+            for i in range(2):
+                n = 2 * c + i
+                nc.vector.tensor_tensor(
+                    out=pages[n][:].indirect(place_list[:, HALF * u // 16 : HALF * (u + 1) // 16]),
+                    in0=scores[i][:],
+                    in1=wgo_sb[:, hops],
+                    op=ALU.mult,
                 )
-            biased = ring.tile([P, width], F32, name="biased")
-            nc.scalar.activation(out=biased[:], in_=ye, func=ACT.Identity, bias=be_cols[:, n : n + 1])
-            score = ring.tile([P, width], F32, name="score")
-            nc.vector.tensor_tensor(out=score[:], in0=yc, in1=biased[:], op=ALU.max)
-            return score
-
-        def place(n, j0, width, score):
-            nc.vector.tensor_tensor(
-                out=pages[n][:].indirect(place_list[:, j0 // 16 : (j0 + width) // 16]),
-                in0=score[:],
-                in1=wgo_sb[:, j0 : j0 + width],
-                op=ALU.mult,
-            )
-            if j0 + width == S:
-                nc.sync.dma_start(out=out[P * n : P * (n + 1), :], in_=pages[n][:])
-
-        def half_step(n, u):
-            shared = bank(2 * u + n)
-            return (n, HALF * u, HALF, readings(n, HALF * u, HALF, shared[:, 0:HALF], shared[:, HALF:S], True))
-
-        def whole_step(n):
-            first = (4 + 2 * (n - 2)) % 8
-            return (n, 0, S, readings(n, 0, S, bank(first)[:], bank(first + 1)[:], False))
+                if u == 1:
+                    nc.sync.dma_start(out=out[P * n : P * (n + 1), :], in_=pages[n][:])
 
         quantize_wc(0, ("scalar", "vector"))
-        pending = half_step(0, 0)
-        later = [
-            lambda: half_step(1, 0),
-            lambda: features(1, 1),
-            lambda: half_step(0, 1),
-            lambda: quantize_wc(1, ("scalar", "scalar")),
-            lambda: half_step(1, 1),
-            lambda: whole_step(2),
-            lambda: quantize_wc(2, ("scalar", "scalar")),
-            lambda: whole_step(3),
-            lambda: whole_step(4),
-            lambda: whole_step(5),
-        ]
-        for step in later:
-            made = step()
-            if made is not None:
-                place(*pending)
-                pending = made
-        place(*pending)
+        for b in range(PASSES):
+            weave_features(b, 1)
+        for b in range(PASSES):
+            quantize_features(b, 1)
+        for c in range(CHUNKS):
+            score_and_place(c, 0)
+            if c + 1 < CHUNKS:
+                quantize_wc(c + 1, ("scalar", "scalar"))
+            score_and_place(c, 1)

@@ -49,10 +49,10 @@ def tile_list_backhaul_hop_planner_kernel(
             return psum.tile([P, 512], F32, name="bank%d" % number)
 
         tab_plane = sb("tab_plane", T, U8)
-        tab_plane1 = sb("tab_plane1", T, U8)
+        near_plane1 = sb("near_plane1", S, U8)
         wa_plane_raw = laid_over("wa_plane_raw", PASSES * H, U8, 1536)
         we_plane = sb("we_plane", N, U8)
-        for plane in (tab_plane, wa_plane_raw, tab_plane1, we_plane):
+        for plane in (tab_plane, wa_plane_raw, near_plane1, we_plane):
             nc.vector.memset(plane[:].bitcast(I32), 0)
         pages = [sb("page%d" % n, T2, F32) for n in range(N // P)]
         for page in pages:
@@ -100,11 +100,6 @@ def tile_list_backhaul_hop_planner_kernel(
             )
         load_tab(1)
         wb_raw[0, 1] = [load_rows("wb_raw01", wb, 1, 0, KP)]
-        for q in range(QUADS):
-            nc.sync.dma_start(
-                out=tab_plane1[32 * q : 32 * q + 4, :].bitcast(I32),
-                in_=tab_scales[1, 4 * q : 4 * q + 4, :].bitcast(I32),
-            )
         wb_raw[1, 0] = [load_rows("wb_raw10", wb, 0, KP, KP, 8192)]
         wb_raw[1, 1] = [load_rows("wb_raw11_%d" % u, wb, 1, KP + u * 256, 256) for u in range(2)]
         bh_cols = sb("bh_cols", 8, F32)
@@ -146,22 +141,22 @@ def tile_list_backhaul_hop_planner_kernel(
         near_plane = sb("near_plane", S, U8)
         nc.vector.tensor_copy(near_plane[:], tab_plane[:].indirect(near_list[:]))
         nc.vector.tensor_copy(far_plane[:], tab_plane[:].indirect(far_list[:]))
-        near_plane1 = sb("near_plane1", S, U8)
         near_planes = [near_plane, near_plane1]
 
         wa_plane = sb("wa_plane", PASSES * H, U8)
         nc.vector.tensor_copy(
-            out=wa_plane[:].rearrange("p (g t m) -> p g m t", t=PACK, m=P),
-            in_=wa_plane_raw[:].rearrange("p (g m t) -> p g m t", t=PACK, m=P),
+            out=wa_plane[:].rearrange("p (g t c i) -> p g c t i", t=PACK, c=8, i=16),
+            in_=wa_plane_raw[:].rearrange("p (g c i t) -> p g c t i", t=PACK, c=8, i=16),
         )
         wa_codes = []
         for a in range(PASSES):
             codes = sb("wa_codes%d" % a, 2 * H, U8)
             nc.scalar.copy(
-                out=codes[:].bitcast(U16).rearrange("p (b t m) -> p b m t", t=PACK, m=P),
-                in_=wa_raw[a][:].bitcast(U16).rearrange("p (b m t) -> p b m t", t=PACK, m=P),
+                out=codes[:].bitcast(U16).rearrange("p (b t c i) -> p b c t i", t=PACK, c=16, i=8),
+                in_=wa_raw[a][:].bitcast(U16).rearrange("p (b c i t) -> p b c t i", t=PACK, c=16, i=8),
             )
             wa_codes.append(codes)
+        nc.scalar.dma_start(out=near_plane1[0:100, :].bitcast(I32), in_=near_plane[4:104, :].bitcast(I32))
 
         near = [sb("near0", S, U32), laid_over("near1", S, U32, 0)]
         far = [sb("far0", S, U32), laid_over("far1", S, U32, 2560)]
@@ -181,14 +176,14 @@ def tile_list_backhaul_hop_planner_kernel(
 
         def quantize_wb(b, a, scalar_share, calls):
             woven = sb("wb_woven%d%d" % (b, a), PACK * KP, BF16, tag="wb_woven%d_bytes" % a)
-            dst = woven[:].rearrange("p (t m j) -> p m j t", t=PACK, j=PACK)
+            dst = woven[:].rearrange("p (t m j) -> p m t j", t=PACK, j=PACK)
             raws = wb_raw[b, a]
             per_raw = P // len(raws)
             for engine, m0, m1 in (("scalar", 0, scalar_share), ("vector", scalar_share, P)):
                 for u, raw in enumerate(raws):
                     lo, hi = max(m0, u * per_raw), min(m1, (u + 1) * per_raw)
                     if lo < hi:
-                        src = raw[:].rearrange("p (j m t) -> p m j t", j=PACK, t=PACK)
+                        src = raw[:].rearrange("p (j m t) -> p m t j", j=PACK, t=PACK)
                         cast(engine, dst[:, lo:hi], src[:, lo - u * per_raw : hi - u * per_raw])
             codes = sb("wb_codes%d%d" % (b, a), KP, U32, tag="wb_codes%d%d_bytes" % (b, a))
             if (b, a) == (0, 0):
@@ -255,13 +250,19 @@ def tile_list_backhaul_hop_planner_kernel(
                     func=ACT.Sin,
                     bias=bh_cols[:, PACK * b + t : PACK * b + t + 1],
                 )
+            rounded = ring.tile([P, PACK * HALF], BF16, name="h_rounded")
+            for t in range(PACK):
+                nc.vector.tensor_scalar(
+                    out=rounded[:, HALF * t : HALF * (t + 1)],
+                    in0=sines[:, HALF * t : HALF * (t + 1)],
+                    scalar1=gain_cols[:, PACK * b + t : PACK * b + t + 1],
+                    scalar2=None,
+                    op0=ALU.mult,
+                )
             woven = sb("h_woven%d%d" % (b, u), PACK * HALF, BF16, tag="h_woven%d%d_bytes" % (b, u))
-            gains = gain_cols[:, PACK * b : PACK * (b + 1)].unsqueeze(1).unsqueeze(3)
-            nc.vector.tensor_tensor(
+            nc.vector.tensor_copy(
                 out=woven[:].rearrange("p (c i t) -> p c t i", i=LINE, t=PACK),
-                in0=sines[:].rearrange("p (t c i) -> p c t i", i=LINE, t=PACK),
-                in1=gains.to_broadcast([P, HALF // LINE, PACK, LINE]),
-                op=ALU.mult,
+                in_=rounded[:].rearrange("p (t c i) -> p c t i", i=LINE, t=PACK),
             )
             h_woven[b, u] = woven
 
@@ -277,7 +278,6 @@ def tile_list_backhaul_hop_planner_kernel(
         quantize_wb(0, 0, P, 1)
         far_passes(0, 0, 0)
         gather_pass(1)
-        nc.vector.tensor_copy(near_plane1[:], tab_plane1[:].indirect(near_list[:]))
         near_passes(0, 1, 0)
         near_passes(1, 1, 0)
         quantize_wb(0, 1, P, 1)

from contextlib import ExitStack

import concourse.mybir as mybir

K, H, N, T, S, T2 = 1024, 1024, 768, 2048, 512, 1024
FLOPS = 2 * 2 * K * H * S + 2 * 2 * H * N * S

F32 = mybir.dt.float32
BF16 = mybir.dt.bfloat16
I32 = mybir.dt.int32
U32 = mybir.dt.uint32
U16 = mybir.dt.uint16
U8 = mybir.dt.uint8
FP8X4 = mybir.dt.float8_e4m3fn_x4
FP4X4 = mybir.dt.float4_e2m1fn_x4
ACT = mybir.ActivationFunctionType
ALU = mybir.AluOpType

P = 128
PACK = 4
KP = P * PACK
PASSES = 2
HALF = S // 2
CHUNK = 256
CHUNKS = N // CHUNK
QUADS = 4
LINE = 4


def tile_list_backhaul_hop_planner_kernel(
    tc, tab_words, tab_scales, offs, offs2, offs3, wa_words, wa_scales, wb, bh, gain, wc,
    we_words, we_scales, be, wgo, out,
):
    nc = tc.nc
    with ExitStack() as ctx:
        lists = ctx.enter_context(tc.tile_pool(name="lists", bufs=1))
        keep = ctx.enter_context(tc.tile_pool(name="keep", bufs=1))
        overlay = ctx.enter_context(tc.tile_pool(name="overlay", bufs=1))
        ring = ctx.enter_context(tc.tile_pool(name="ring", bufs=3))
        psum = ctx.enter_context(tc.psum_pool(name="psum", bufs=1))

        def sb(name, cols, dtype, tag=""):
            return keep.tile([P, cols], dtype, name=name, tag=tag, align_bytes=64)

        def laid_over(name, cols, dtype, offset):
            return overlay.tile([P, cols], dtype, name=name, offset=offset, align_bytes=64)

        def bank(number):
            return psum.tile([P, 512], F32, name="bank%d" % number)

        tab_plane = sb("tab_plane", T, U8)
        near_plane1 = sb("near_plane1", S, U8)
        wa_plane_raw = laid_over("wa_plane_raw", PASSES * H, U8, 1536)
        we_plane = sb("we_plane", N, U8)
        for plane in (tab_plane, wa_plane_raw, near_plane1, we_plane):
            nc.vector.memset(plane[:].bitcast(I32), 0)
        pages = [sb("page%d" % n, T2, F32) for n in range(N // P)]
        for page in pages:
            nc.vector.memset(page[:].bitcast(I32), 0)

        near_list = lists.tile([P, S // 16], U16, name="near_list")
        far_list = lists.tile([P, S // 16], U16, name="far_list")
        place_list = lists.tile([P, S // 16], U16, name="place_list")
        tab = [sb("tab%d" % a, T, U32) for a in range(PASSES)]

        def load_tab(a):
            nc.sync.dma_start(
                out=tab[a][:].bitcast(I32),
                in_=tab_words[a].rearrange("p t i -> p (t i)").bitcast(I32),
            )

        def load_rows(name, w, a, c0, width, offset=None):
            if offset is None:
                raw = sb(name, PACK * width, F32)
            else:
                raw = laid_over(name, PACK * width, F32, offset)
            nc.sync.dma_start(
                out=raw[:].rearrange("p (j c) -> p j c", j=PACK),
                in_=w[KP * a : KP * (a + 1), c0 : c0 + width].rearrange("(p j) c -> p j c", j=PACK),
            )
            return raw

        nc.sync.dma_start(near_list[:], offs)
        nc.sync.dma_start(far_list[:], offs2)
        load_tab(0)
        wa_raw = [sb("wa_raw%d" % a, 2 * H, U8) for a in range(PASSES)]
        for a in range(PASSES):
            nc.sync.dma_start(out=wa_raw[a][:].bitcast(I32), in_=wa_words[a].bitcast(I32))
        for q in range(QUADS):
            nc.sync.dma_start(
                out=tab_plane[32 * q : 32 * q + 8, :].bitcast(I32),
                in_=tab_scales[:, 4 * q : 4 * q + 4, :].bitcast(I32),
            )
        wb_raw = {}
        wb_raw[0, 0] = [load_rows("wb_raw00", wb, 0, 0, KP)]
        for q in range(QUADS):
            nc.sync.dma_start(
                out=wa_plane_raw[32 * q : 32 * q + 4, :].bitcast(I32).rearrange("r (a c) -> r a c", a=PASSES),
                in_=wa_scales[:, 4 * q : 4 * q + 4, :].bitcast(I32).rearrange("a r c -> r a c"),
            )
        load_tab(1)
        wb_raw[0, 1] = [load_rows("wb_raw01", wb, 1, 0, KP)]
        wb_raw[1, 0] = [load_rows("wb_raw10", wb, 0, KP, KP, 8192)]
        wb_raw[1, 1] = [load_rows("wb_raw11_%d" % u, wb, 1, KP + u * 256, 256) for u in range(2)]
        bh_cols = sb("bh_cols", 8, F32)
        gain_cols = sb("gain_cols", 8, F32)
        for cols, vec in ((bh_cols, bh), (gain_cols, gain)):
            nc.sync.dma_start(
                out=cols[:].rearrange("p (b t) -> p b t", t=PACK),
                in_=vec.rearrange("(b p t) -> p b t", p=P, t=PACK),
            )

        we_codes = []
        wc_raw = []

        def load_chunk(c):
            codes = sb("we_codes%d" % c, PASSES * CHUNK, U32)
            nc.sync.dma_start(
                out=codes[:].bitcast(I32).rearrange("p (a c) -> p a c", a=PASSES),
                in_=we_words[:, :, CHUNK * c : CHUNK * (c + 1), :].rearrange("a p c i -> p a (c i)").bitcast(I32),
            )
            we_codes.append(codes)
            wc_raw.append([load_rows("wc_raw%d%d" % (c, a), wc, a, CHUNK * c, CHUNK) for a in range(PASSES)])

        for q in range(QUADS):
            nc.sync.dma_start(
                out=we_plane[32 * q : 32 * q + 8, :].bitcast(I32),
                in_=we_scales[:, 4 * q : 4 * q + 4, :].bitcast(I32),
            )
        load_chunk(0)
        nc.sync.dma_start(place_list[:], offs3)
        be_cols = sb("be_cols", N // P, F32)
        with nc.allow_non_contiguous_dma(reason="one bias value for each partition and tile of rows"):
            nc.sync.dma_start(out=be_cols[:], in_=be.rearrange("(n p) -> p n", p=P))
        wgo_sb = sb("wgo_sb", S, F32)
        nc.sync.dma_start(out=wgo_sb[:], in_=wgo)
        for c in range(1, CHUNKS):
            load_chunk(c)

        far_plane = sb("far_plane", S, U8)
        near_plane = sb("near_plane", S, U8)
        nc.vector.tensor_copy(near_plane[:], tab_plane[:].indirect(near_list[:]))
        nc.vector.tensor_copy(far_plane[:], tab_plane[:].indirect(far_list[:]))
        near_planes = [near_plane, near_plane1]

        wa_plane = sb("wa_plane", PASSES * H, U8)
        nc.vector.tensor_copy(
            out=wa_plane[:].rearrange("p (g t c i) -> p g c t i", t=PACK, c=8, i=16),
            in_=wa_plane_raw[:].rearrange("p (g c i t) -> p g c t i", t=PACK, c=8, i=16),
        )
        wa_codes = []
        for a in range(PASSES):
            codes = sb("wa_codes%d" % a, 2 * H, U8)
            nc.scalar.copy(
                out=codes[:].bitcast(U16).rearrange("p (b t c i) -> p b c t i", t=PACK, c=16, i=8),
                in_=wa_raw[a][:].bitcast(U16).rearrange("p (b c i t) -> p b c t i", t=PACK, c=16, i=8),
            )
            wa_codes.append(codes)
        nc.scalar.dma_start(out=near_plane1[0:100, :].bitcast(I32), in_=near_plane[4:104, :].bitcast(I32))

        near = [sb("near0", S, U32), laid_over("near1", S, U32, 0)]
        far = [sb("far0", S, U32), laid_over("far1", S, U32, 2560)]

        def gather_pass(a):
            nc.vector.tensor_copy(near[a][:], tab[a][:].indirect(near_list[:]))
            nc.vector.tensor_copy(far[a][:], tab[a][:].indirect(far_list[:]))

        def cast(engine, out_ap, in_ap):
            if engine == "scalar":
                nc.scalar.copy(out=out_ap, in_=in_ap)
            else:
                nc.vector.tensor_copy(out=out_ap, in_=in_ap)

        wb_codes = {}
        wb_planes = {}

        def quantize_wb(b, a, scalar_share, calls):
            woven = sb("wb_woven%d%d" % (b, a), PACK * KP, BF16, tag="wb_woven%d_bytes" % a)
            dst = woven[:].rearrange("p (t m j) -> p m t j", t=PACK, j=PACK)
            raws = wb_raw[b, a]
            per_raw = P // len(raws)
            for engine, m0, m1 in (("scalar", 0, scalar_share), ("vector", scalar_share, P)):
                for u, raw in enumerate(raws):
                    lo, hi = max(m0, u * per_raw), min(m1, (u + 1) * per_raw)
                    if lo < hi:
                        src = raw[:].rearrange("p (j m t) -> p m t j", j=PACK, t=PACK)
                        cast(engine, dst[:, lo:hi], src[:, lo - u * per_raw : hi - u * per_raw])
            codes = sb("wb_codes%d%d" % (b, a), KP, U32, tag="wb_codes%d%d_bytes" % (b, a))
            if (b, a) == (0, 0):
                plane = laid_over("wb_plane00", KP, U8, 2048)
            else:
                plane = sb("wb_plane%d%d" % (b, a), KP, U8)
            width = KP // calls
            for i in range(calls):
                cols = slice(i * width, (i + 1) * width)
                nc.vector.quantize_mx(
                    out=codes[:, cols].bitcast(FP8X4),
                    scales=plane[:, cols],
                    in_=woven[:, PACK * i * width : PACK * (i + 1) * width],
                )
            wb_codes[b, a] = codes
            wb_planes[b, a] = plane

        sums = {(b, u, tp): bank(4 * b + 2 * u + tp) for b in range(PASSES) for u in range(2) for tp in range(2)}

        def near_passes(b, a, u):
            if True:
                hops = slice(HALF * u, HALF * (u + 1))
                for t in range(PACK):
                    c0 = KP * b + P * t
                    nc.tensor.matmul_mx(
                        out=sums[b, u, t // 2][:, HALF * (t % 2) : HALF * (t % 2 + 1)],
                        lhsT=wa_codes[a][:, 2 * c0 : 2 * (c0 + P)].bitcast(FP4X4),
                        lhsT_scale=wa_plane[:, H * a + c0 : H * a + c0 + P],
                        rhs=near[a][:, hops].bitcast(FP8X4),
                        rhs_scale=near_planes[a][:, hops],
                        start=(a == 0 and t % 2 == 0),
                        stop=False,
                    )

        def far_passes(b, a, u):
            if True:
                hops = slice(HALF * u, HALF * (u + 1))
                for t in range(PACK):
                    cols = slice(P * t, P * (t + 1))
                    nc.tensor.matmul_mx(
                        out=sums[b, u, t // 2][:, HALF * (t % 2) : HALF * (t % 2 + 1)],
                        lhsT=wb_codes[b, a][:, cols].bitcast(FP8X4),
                        lhsT_scale=wb_planes[b, a][:, cols],
                        rhs=far[a][:, hops].bitcast(FP8X4),
                        rhs_scale=far_plane[4 * a : P, hops],
                        start=False,
                        stop=(a == PASSES - 1 and t % 2 == 1),
                    )

        h_codes = [sb("h_codes%d" % b, S, U32) for b in range(PASSES)]
        h_planes = [sb("h_plane%d" % b, S, U8) for b in range(PASSES)]

        h_woven = {}

        def weave_features(b, u):
            if b == 0:
                sines = laid_over("sines0%d" % u, PACK * HALF, F32, 8192 + 4096 * u)
            else:
                sines = sb("sines1%d" % u, PACK * HALF, F32, tag="sines1%d_bytes" % u)
            for t in range(PACK):
                nc.scalar.activation(
                    out=sines[:, HALF * t : HALF * (t + 1)],
                    in_=sums[b, u, t // 2][:, HALF * (t % 2) : HALF * (t % 2 + 1)],
                    func=ACT.Sin,
                    bias=bh_cols[:, PACK * b + t : PACK * b + t + 1],
                )
            rounded = ring.tile([P, PACK * HALF], BF16, name="h_rounded")
            for t in range(PACK):
                nc.vector.tensor_scalar(
                    out=rounded[:, HALF * t : HALF * (t + 1)],
                    in0=sines[:, HALF * t : HALF * (t + 1)],
                    scalar1=gain_cols[:, PACK * b + t : PACK * b + t + 1],
                    scalar2=None,
                    op0=ALU.mult,
                )
            woven = sb("h_woven%d%d" % (b, u), PACK * HALF, BF16, tag="h_woven%d%d_bytes" % (b, u))
            nc.vector.tensor_copy(
                out=woven[:].rearrange("p (c i t) -> p c t i", i=LINE, t=PACK),
                in_=rounded[:].rearrange("p (t c i) -> p c t i", i=LINE, t=PACK),
            )
            h_woven[b, u] = woven

        def quantize_features(b, u):
            hops = slice(HALF * u, HALF * (u + 1))
            nc.vector.quantize_mx(
                out=h_codes[b][:, hops].bitcast(FP8X4), scales=h_planes[b][:, hops], in_=h_woven[b, u][:]
            )

        gather_pass(0)
        near_passes(0, 0, 0)
        near_passes(1, 0, 0)
        quantize_wb(0, 0, P, 1)
        far_passes(0, 0, 0)
        gather_pass(1)
        near_passes(0, 1, 0)
        near_passes(1, 1, 0)
        quantize_wb(0, 1, P, 1)
        far_passes(0, 1, 0)
        quantize_wb(1, 0, P, 1)
        far_passes(1, 0, 0)
        quantize_wb(1, 1, 0, PACK)
        far_passes(1, 1, 0)
        for b in range(PASSES):
            weave_features(b, 0)
        for b in range(PASSES):
            quantize_features(b, 0)
        for b in range(PASSES):
            for a in range(PASSES):
                near_passes(b, a, 1)
                far_passes(b, a, 1)

        wc_codes = {}
        wc_planes = {}
        woven_tags = {
            (0, 0): "",
            (0, 1): "",
            (1, 0): "sines10_bytes",
            (1, 1): "sines11_bytes",
            (2, 0): "h_woven01_bytes",
            (2, 1): "h_woven11_bytes",
        }
        score_tags = {
            (0, 0): "h_woven01_bytes",
            (1, 0): "h_woven11_bytes",
            (0, 1): "sines10_bytes",
            (1, 1): "sines11_bytes",
            (2, 1): "h_woven01_bytes",
            (3, 1): "h_woven11_bytes",
        }

        def quantize_wc(c, engines):
            for a in range(PASSES):
                if True:
                    woven = sb("wc_woven%d%d" % (c, a), PACK * CHUNK, BF16, tag=woven_tags[c, a])
                cast(
                    engines[a],
                    woven[:].rearrange("p (c i j) -> p c j i", i=LINE, j=PACK),
                    wc_raw[c][a][:].rearrange("p (j c i) -> p c j i", i=LINE, j=PACK),
                )
                codes = sb("wc_codes%d%d" % (c, a), CHUNK, U32)
                plane = sb("wc_plane%d%d" % (c, a), CHUNK, U8)
                nc.vector.quantize_mx(out=codes[:].bitcast(FP8X4), scales=plane[:], in_=woven[:])
                wc_codes[c, a] = codes
                wc_planes[c, a] = plane

        def score_and_place(c, u):
            hops = slice(HALF * u, HALF * (u + 1))
            first_bank = (2 * (2 * c + u)) % 8
            ye, yc = bank(first_bank), bank(first_bank + 1)
            for a in range(PASSES):
                for i in range(2):
                    n, cols = 2 * c + i, slice(P * i, P * (i + 1))
                    first, last = (a == 0 and i == 0), (a == PASSES - 1 and i == 1)
                    nc.tensor.matmul_mx(
                        out=yc[:, HALF * i : HALF * (i + 1)],
                        lhsT=wc_codes[c, a][:, cols].bitcast(FP8X4),
                        lhsT_scale=wc_planes[c, a][:, cols],
                        rhs=h_codes[a][:, hops].bitcast(FP8X4),
                        rhs_scale=h_planes[a][:, hops],
                        start=first,
                        stop=last,
                    )
                for i in range(2):
                    n, cols = 2 * c + i, slice(P * i, P * (i + 1))
                    first, last = (a == 0 and i == 0), (a == PASSES - 1 and i == 1)
                    nc.tensor.matmul_mx(
                        out=ye[:, HALF * i : HALF * (i + 1)],
                        lhsT=we_codes[c][:, CHUNK * a + cols.start : CHUNK * a + cols.stop].bitcast(FP8X4),
                        lhsT_scale=we_plane[4 * a : P, P * n : P * (n + 1)],
                        rhs=h_codes[a][:, hops].bitcast(FP8X4),
                        rhs_scale=h_planes[a][:, hops],
                        start=first,
                        stop=last,
                    )
            yc_sb = ring.tile([P, S], F32, name="yc_sb")
            nc.scalar.copy(out=yc_sb[:], in_=yc[:])
            scores = []
            for i in range(2):
                n = 2 * c + i
                score = sb("score%d%d" % (n, u), HALF, F32, tag=score_tags.get((n, u), ""))
                nc.vector.scalar_tensor_tensor(
                    out=score[:],
                    in0=ye[:, HALF * i : HALF * (i + 1)],
                    scalar=be_cols[:, n : n + 1],
                    in1=yc_sb[:, HALF * i : HALF * (i + 1)],
                    op0=ALU.add,
                    op1=ALU.max,
                )
                scores.append(score)
            for i in range(2):
                n = 2 * c + i
                nc.vector.tensor_tensor(
                    out=pages[n][:].indirect(place_list[:, HALF * u // 16 : HALF * (u + 1) // 16]),
                    in0=scores[i][:],
                    in1=wgo_sb[:, hops],
                    op=ALU.mult,
                )
                if u == 1:
                    nc.sync.dma_start(out=out[P * n : P * (n + 1), :], in_=pages[n][:])

        quantize_wc(0, ("scalar", "vector"))
        for b in range(PASSES):
            weave_features(b, 1)
        for b in range(PASSES):
            quantize_features(b, 1)
        for c in range(CHUNKS):
            score_and_place(c, 0)
            if c + 1 < CHUNKS:
                quantize_wc(c + 1, ("scalar", "scalar"))
            score_and_place(c, 1)
